import numpy as np, ml_dtypes
CORES = [16,32,48,64,80]
N = 5
QP = 128
def setup_inputs(rng):
    return {"q": rng.standard_normal((N, 128, QP), dtype=np.float32).astype(ml_dtypes.bfloat16), "k": rng.standard_normal((N, 128, 128), dtype=np.float32).astype(ml_dtypes.bfloat16), "v": rng.standard_normal((N, 128, 128), dtype=np.float32).astype(ml_dtypes.bfloat16)}
def setup_inputs_big(rng):
    d = setup_inputs(rng)
    for k in ("q", "k", "v"): d[k] = (d[k].astype(np.float32) * 1024.0).astype(d[k].dtype)
    return d
def setup_inputs_small(rng):
    d = setup_inputs(rng)
    for k in ("q", "k", "v"): d[k] = (d[k].astype(np.float32) * (1 / 1024.0)).astype(d[k].dtype)
    return d
def setup_inputs_apart(rng):
    d = setup_inputs(rng)
    f = (10.0 ** rng.permutation(np.linspace(-1.5, 1.5, N))).astype(np.float32).reshape(N, 1, 1)
    for k in ("q", "k", "v"): d[k] = (d[k].astype(np.float32) * f).astype(d[k].dtype)
    return d
def reference(q, k, v):
    Q, K, V = q.astype(np.float64), k.astype(np.float64), v.astype(np.float64)
    y = np.zeros((N, 128, QP))
    for r in range(N):
        S = [K[j].T @ Q[r] for j in range(N)]
        m = np.max([s.max(axis=0) for s in S], axis=0)
        y[r] = sum(V[j].T @ np.maximum(S[j] - 0.5 * m, 0.0) for j in range(N))
    return {"y": y.astype(ml_dtypes.bfloat16)}

@@ -1,0 +1,193 @@
+from concourse.bass import DstId, RemoteDMATransfer
+from concourse.mybir import AluOpType
+
+N = 5
+W = 128
+H = W // 2
+PACK = False
+
+SCRATCH = {
+    "kv": ("sbuf", [128, N * 2 * W], "bfloat16"),
+    "qs": ("sbuf", [128, W], "bfloat16"),
+    "ida": ("sbuf", [128, W + 1], "bfloat16"),
+    "dg": ("dram", [W + 1, 128], "bfloat16"),
+    "idn": ("sbuf", [128, W], "bfloat16"),
+    "zero": ("sbuf", [128, W], "float32"),
+    "ones": ("sbuf", [128, W], "bfloat16"),
+    "run": ("sbuf", [128, 2 * N * H], "float32"),
+    "tree": ("sbuf", [128, H], "float32"),
+    "mcol": ("sbuf", [128, 8], "bfloat16"),
+    "mrow": ("sbuf", [128, W], "bfloat16"),
+    "p": ("sbuf", [128, N * W], "bfloat16"),
+    "ysb": ("sbuf", [128, W], "bfloat16"),
+    "ps0": ("psum", [128, 512], "float32"),
+    "ps1": ("psum", [128, 512], "float32"),
+    "ps2": ("psum", [128, 512], "float32"),
+    "ps3": ("psum", [128, 512], "float32"),
+    "ps4": ("psum", [128, 512], "float32"),
+    "sta": ("psum", [128, 512], "float32"),
+    "stb": ("psum", [128, 512], "float32"),
+    "yp": ("psum", [128, 512], "float32"),
+}
+SEMAPHORES = (["k%d" % d for d in range(1, N)] + ["v%d" % d for d in range(1, N)] + ["snt"]
+              + ["c%d" % i for i in range(64)])
+
+
+def rank_program(g, core, T, topo):
+    rank = T.rank_of(core)
+    if rank is None:
+        return
+    pe, dve, sy, sc = g.tensor, g.vector, g.sync, g.scalar
+    cnt = [0]
+
+    def new():
+        s = T.sem["c%d" % cnt[0]]
+        cnt[0] += 1
+        return s
+
+    def kcols(d):
+        return slice(d * 2 * W, d * 2 * W + W)
+
+    def vcols(d):
+        return slice(d * 2 * W + W, (d + 1) * 2 * W)
+
+    def kvcols(d):
+        return slice(d * 2 * W, (d + 1) * 2 * W)
+
+    kv, qs = T.kv, T.qs
+    S = [T.ps0, T.ps1, T.ps2, T.ps3, T.ps4]
+    ST = [T.sta, T.stb]
+
+    ldk, ldv, ldq = new(), new(), new()
+    sy.dma_start(kv[:, kcols(0)], T.k[:, :]).then_inc(ldk, 16)
+    sc.dma_start(kv[:, vcols(0)], T.v[:, :]).then_inc(ldv, 16)
+    sc.dma_start(qs[:, :], T.q[:, :]).then_inc(ldq, 16)
+
+    a1, a2, one_s, zero_s, idw, idl = new(), new(), new(), new(), new(), new()
+    dve.memset(T.ida[:, 0:1], -0.5).then_inc(a1, 1)
+    dve.memset(T.ida[:, 1:W + 1], 0.0).then_inc(a2, 1)
+    dve.memset(T.ones[0:1, :], 1.0).then_inc(one_s, 1)
+    dve.memset(T.zero[:, :], 0.0).then_inc(zero_s, 1)
+    sy.wait_ge(a1, 1)
+    sy.wait_ge(a2, 1)
+    sy.dma_start(T.dg[:, :], T.ida[:, :]).then_inc(idw, 16)
+    sy.wait_ge(idw, 16)
+    sy.dma_start(T.idn[:, :], T.dg[0:W, :]).then_inc(idl, 16)
+
+    peers = [(d, T.cores[(rank + d) % N]) for d in range(1, N)]
+    common = topo.mask(core, peers[0][1])
+    for _, c in peers:
+        common &= topo.mask(core, c)
+    engines = [e for e in range(16) if (common >> e) & 1]
+    ne = len(engines) // len(peers)
+
+    def send(cols_of, semname):
+        trs = []
+        for i, (d, c) in enumerate(peers):
+            rid, pid, _ = topo.addr(c)
+            m = 0
+            for e in engines[i * ne:(i + 1) * ne]:
+                m |= 1 << e
+            trs.append(RemoteDMATransfer(dst_ids=[DstId(rid=rid, pnc=pid)], dma_engine_mask=m,
+                                         remote_sem=T.sem["%s%d" % (semname, d)],
+                                         src=kv[:, cols_of(0)], dst=kv[:, cols_of(d)]))
+        g.remote_dma_fused(trs, local_sem=T.sem.snt)
+        return ne * len(peers)
+
+    sent = 0
+    g.wait_ge(ldk, 16)
+    if PACK:
+        g.wait_ge(ldv, 16)
+        sent += send(kvcols, "k")
+    else:
+        sent += send(kcols, "k")
+        g.wait_ge(ldv, 16)
+        sent += send(vcols, "v")
+    g.wait_ge(T.sem.snt, sent)
+
+    pe.wait_ge(ldk, 16)
+    pe.wait_ge(ldq, 16)
+    rd = [None] * N
+    prev = None
+    for d in range(N):
+        if d:
+            pe.wait_ge(T.sem["k%d" % d], ne)
+        if d >= 2:
+            pe.wait_ge(rd[d - 2], 1)
+        s = new()
+        pe.matmul(ST[d % 2][:, 0:W], lhsT=qs[:, :], rhs=kv[:, kcols(d)], start=True, stop=True).then_inc(s, 1)
+        pe.matmul(S[d][:, 0:W], lhsT=kv[:, kcols(d)], rhs=qs[:, :], start=True, stop=False)
+        dve.wait_ge(s, 1)
+        for h in range(2):
+            off = (2 * d + h) * H
+            t = new()
+            if prev is None:
+                dve.tensor_copy(T.run[:, off:off + H], ST[d % 2][:, h * H:(h + 1) * H]).then_inc(t, 1)
+            else:
+                dve.wait_ge(prev[1], 1)
+                dve.tensor_tensor(T.run[:, off:off + H], ST[d % 2][:, h * H:(h + 1) * H],
+                                  T.run[:, prev[0]:prev[0] + H], AluOpType.max).then_inc(t, 1)
+            prev = (off, t)
+        rd[d] = prev[1]
+
+    src, so, sem = T.run, prev[0], prev[1]
+    to = 0
+    w = H // 2
+    while w >= 1:
+        t = new()
+        dve.wait_ge(sem, 1)
+        out = T.tree[:, to:to + w] if w > 1 else T.mcol[:, 0:1]
+        dve.tensor_tensor(out, src[:, so:so + w], src[:, so + w:so + 2 * w], AluOpType.max).then_inc(t, 1)
+        src, so, sem = T.tree, to, t
+        to += w
+        w //= 2
+
+    mr, mw = new(), new()
+    pe.wait_ge(idl, 16)
+    pe.wait_ge(one_s, 1)
+    pe.wait_ge(sem, 1)
+    pe.matmul(T.stb[0:1, 0:W], lhsT=T.mcol[:, 0:1], rhs=T.idn[:, :], start=True, stop=True).then_inc(mr, 1)
+    dve.wait_ge(zero_s, 1)
+    dve.wait_ge(mr, 1)
+    dve.tensor_copy(T.mrow[0:1, :], T.stb[0:1, 0:W]).then_inc(mw, 1)
+    pe.wait_ge(mw, 1)
+
+    bs = [new() for _ in range(N)]
+    rs = [new() for _ in range(N)]
+    yd, yc, stq = new(), new(), new()
+
+    def bias(d):
+        pe.matmul(S[d][:, 0:W], lhsT=T.ones[0:1, :], rhs=T.mrow[0:1, :], start=False, stop=True).then_inc(bs[d], 1)
+
+    def pv(d):
+        pe.wait_ge(rs[d], 1)
+        if d == 0:
+            pe.wait_ge(ldv, 16)
+        elif not PACK:
+            pe.wait_ge(T.sem["v%d" % d], ne)
+        i = pe.matmul(T.yp[:, 0:W], lhsT=kv[:, vcols(d)], rhs=T.p[:, d * W:(d + 1) * W],
+                      start=(d == 0), stop=(d == N - 1))
+        if d == N - 1:
+            i.then_inc(yd, 1)
+
+    for d in range(N):
+        dve.wait_ge(bs[d], 1)
+        dve.tensor_tensor(T.p[:, d * W:(d + 1) * W], S[d][:, 0:W], T.zero[:, :], AluOpType.max).then_inc(rs[d], 1)
+    if PACK:
+        bias(0)
+        bias(1)
+        for d in range(N):
+            if d + 2 < N:
+                bias(d + 2)
+            pv(d)
+    else:
+        for d in range(N):
+            bias(d)
+        for d in range(N):
+            pv(d)
+
+    dve.wait_ge(yd, 1)
+    dve.tensor_copy(T.ysb[:, :], T.yp[:, 0:W]).then_inc(yc, 1)
+    sy.wait_ge(yc, 1)
+    sy.dma_start(T.y[:, :], T.ysb[:, :]).then_inc(stq, 16)
+    sy.wait_ge(stq, 16)

@@ -4,10 +4,15 @@ from concourse.mybir import AluOpType
 N = 5
 W = 128
 H = W // 2
-PACK = False
+SIM = 96
+KGROUPS = [[1, 2], [3], [4]]
+VGROUPS = [[1, 2], [3, 4]]
+HOPE = 4
+HOP_AFTER = 1
 
 SCRATCH = {
     "kv": ("sbuf", [128, N * 2 * W], "bfloat16"),
+    "hv": ("sbuf", [128, W], "bfloat16"),
     "qs": ("sbuf", [128, W], "bfloat16"),
     "ida": ("sbuf", [128, W + 1], "bfloat16"),
     "dg": ("dram", [W + 1, 128], "bfloat16"),
@@ -29,13 +34,70 @@ SCRATCH = {
     "stb": ("psum", [128, 512], "float32"),
     "yp": ("psum", [128, 512], "float32"),
 }
-SEMAPHORES = (["k%d" % d for d in range(1, N)] + ["v%d" % d for d in range(1, N)] + ["snt"]
-              + ["c%d" % i for i in range(64)])
+SEMAPHORES = (["k%d" % d for d in range(1, N)] + ["v%d" % d for d in range(1, N)] + ["snt", "vin"]
+              + ["c%d" % i for i in range(80)])
+
+
+def bits(m):
+    return [e for e in range(16) if (m >> e) & 1]
+
+
+def tomask(es):
+    m = 0
+    for e in es:
+        m |= 1 << e
+    return m
+
+
+def helpers_of(c, T, topo):
+    hs = [h for h in range(SIM) if h != c and topo.chip(h) == topo.chip(c) and topo.die(h) != topo.die(c)
+          and all(topo.may_write(h, x) for x in T.cores)]
+    return hs[:len(VGROUPS)]
+
+
+def off_chip(core, T, topo):
+    m = None
+    for c in T.cores:
+        if topo.chip(c) != topo.chip(core):
+            m = topo.mask(core, c) if m is None else m & topo.mask(core, c)
+    return m
+
+
+def share(group, core, T, topo):
+    return len(bits(off_chip(core, T, topo))) // len(group)
+
+
+def fan_out(g, T, topo, core, rank, src, cols_of, semname, group):
+    engines = bits(off_chip(core, T, topo))
+    ne = len(engines) // len(group)
+    trs = []
+    for i, d in enumerate(group):
+        rid, pid, _ = topo.addr(T.cores[(rank + d) % N])
+        trs.append(RemoteDMATransfer(dst_ids=[DstId(rid=rid, pnc=pid)],
+                                     dma_engine_mask=tomask(engines[i * ne:(i + 1) * ne]),
+                                     remote_sem=T.sem["%s%d" % (semname, d)],
+                                     src=src, dst=T.kv[:, cols_of(d)]))
+    g.remote_dma_fused(trs, local_sem=T.sem.snt)
+    return ne * len(group)
+
+
+def kcols(d):
+    return slice(d * 2 * W, d * 2 * W + W)
+
+
+def vcols(d):
+    return slice(d * 2 * W + W, (d + 1) * 2 * W)
 
 
 def rank_program(g, core, T, topo):
     rank = T.rank_of(core)
     if rank is None:
+        for r, c in enumerate(T.cores):
+            hs = helpers_of(c, T, topo)
+            if core in hs:
+                g.wait_ge(T.sem.vin, HOPE)
+                n = fan_out(g, T, topo, core, r, T.hv[:, :], vcols, "v", VGROUPS[hs.index(core)])
+                g.wait_ge(T.sem.snt, n)
         return
     pe, dve, sy, sc = g.tensor, g.vector, g.sync, g.scalar
     cnt = [0]
@@ -45,18 +107,17 @@ def rank_program(g, core, T, topo):
         cnt[0] += 1
         return s
 
-    def kcols(d):
-        return slice(d * 2 * W, d * 2 * W + W)
-
-    def vcols(d):
-        return slice(d * 2 * W + W, (d + 1) * 2 * W)
-
-    def kvcols(d):
-        return slice(d * 2 * W, (d + 1) * 2 * W)
-
     kv, qs = T.kv, T.qs
     S = [T.ps0, T.ps1, T.ps2, T.ps3, T.ps4]
     ST = [T.sta, T.stb]
+    Y = [T.yp, T.sta]
+    kn, vn = {}, {}
+    for grp in KGROUPS:
+        for d in grp:
+            kn[d] = share(grp, core, T, topo)
+    for grp in VGROUPS:
+        for d in grp:
+            vn[d] = share(grp, core, T, topo)
 
     ldk, ldv, ldq = new(), new(), new()
     sy.dma_start(kv[:, kcols(0)], T.k[:, :]).then_inc(ldk, 16)
@@ -74,35 +135,22 @@ def rank_program(g, core, T, topo):
     sy.wait_ge(idw, 16)
     sy.dma_start(T.idn[:, :], T.dg[0:W, :]).then_inc(idl, 16)
 
-    peers = [(d, T.cores[(rank + d) % N]) for d in range(1, N)]
-    common = topo.mask(core, peers[0][1])
-    for _, c in peers:
-        common &= topo.mask(core, c)
-    engines = [e for e in range(16) if (common >> e) & 1]
-    ne = len(engines) // len(peers)
-
-    def send(cols_of, semname):
-        trs = []
-        for i, (d, c) in enumerate(peers):
-            rid, pid, _ = topo.addr(c)
-            m = 0
-            for e in engines[i * ne:(i + 1) * ne]:
-                m |= 1 << e
-            trs.append(RemoteDMATransfer(dst_ids=[DstId(rid=rid, pnc=pid)], dma_engine_mask=m,
-                                         remote_sem=T.sem["%s%d" % (semname, d)],
-                                         src=kv[:, cols_of(0)], dst=kv[:, cols_of(d)]))
-        g.remote_dma_fused(trs, local_sem=T.sem.snt)
-        return ne * len(peers)
-
+    hs = helpers_of(core, T, topo)
+    inner = bits(topo.mask(core, hs[0]) & ~off_chip(core, T, topo))
+    hop = []
+    for i, hc in enumerate(hs):
+        rid, pid, _ = topo.addr(hc)
+        hop.append(RemoteDMATransfer(dst_ids=[DstId(rid=rid, pnc=pid)],
+                                     dma_engine_mask=tomask(inner[i * HOPE:(i + 1) * HOPE]),
+                                     remote_sem=T.sem.vin, src=kv[:, vcols(0)], dst=T.hv[:, :]))
     sent = 0
     g.wait_ge(ldk, 16)
-    if PACK:
-        g.wait_ge(ldv, 16)
-        sent += send(kvcols, "k")
-    else:
-        sent += send(kcols, "k")
-        g.wait_ge(ldv, 16)
-        sent += send(vcols, "v")
+    for n, grp in enumerate(KGROUPS):
+        if n == HOP_AFTER:
+            g.wait_ge(ldv, 16)
+            g.remote_dma_fused(hop, local_sem=T.sem.snt)
+            sent += HOPE * len(hs)
+        sent += fan_out(g, T, topo, core, rank, kv[:, kcols(0)], kcols, "k", grp)
     g.wait_ge(T.sem.snt, sent)
 
     pe.wait_ge(ldk, 16)
@@ -111,7 +159,7 @@ def rank_program(g, core, T, topo):
     prev = None
     for d in range(N):
         if d:
-            pe.wait_ge(T.sem["k%d" % d], ne)
+            pe.wait_ge(T.sem["k%d" % d], kn[d])
         if d >= 2:
             pe.wait_ge(rd[d - 2], 1)
         s = new()
@@ -152,42 +200,37 @@ def rank_program(g, core, T, topo):
     dve.tensor_copy(T.mrow[0:1, :], T.stb[0:1, 0:W]).then_inc(mw, 1)
     pe.wait_ge(mw, 1)
 
-    bs = [new() for _ in range(N)]
-    rs = [new() for _ in range(N)]
-    yd, yc, stq = new(), new(), new()
+    rs = {}
+    for d in range(N):
+        b = new()
+        pe.matmul(S[d][:, 0:W], lhsT=T.ones[0:1, :], rhs=T.mrow[0:1, :], start=False, stop=True).then_inc(b, 1)
+        dve.wait_ge(b, 1)
+        parts = [(0, W)] if d < N - 1 else [(0, H), (H, W)]
+        rs[d] = []
+        for lo, hi in parts:
+            r = new()
+            dve.tensor_tensor(T.p[:, d * W + lo:d * W + hi], S[d][:, lo:hi], T.zero[:, lo:hi],
+                              AluOpType.max).then_inc(r, 1)
+            rs[d].append(r)
 
-    def bias(d):
-        pe.matmul(S[d][:, 0:W], lhsT=T.ones[0:1, :], rhs=T.mrow[0:1, :], start=False, stop=True).then_inc(bs[d], 1)
-
-    def pv(d):
-        pe.wait_ge(rs[d], 1)
+    yd = [new(), new()]
+    yc = [new(), new()]
+    stq = new()
+    for d in range(N):
         if d == 0:
             pe.wait_ge(ldv, 16)
-        elif not PACK:
-            pe.wait_ge(T.sem["v%d" % d], ne)
-        i = pe.matmul(T.yp[:, 0:W], lhsT=kv[:, vcols(d)], rhs=T.p[:, d * W:(d + 1) * W],
-                      start=(d == 0), stop=(d == N - 1))
-        if d == N - 1:
-            i.then_inc(yd, 1)
-
-    for d in range(N):
-        dve.wait_ge(bs[d], 1)
-        dve.tensor_tensor(T.p[:, d * W:(d + 1) * W], S[d][:, 0:W], T.zero[:, :], AluOpType.max).then_inc(rs[d], 1)
-    if PACK:
-        bias(0)
-        bias(1)
-        for d in range(N):
-            if d + 2 < N:
-                bias(d + 2)
-            pv(d)
-    else:
-        for d in range(N):
-            bias(d)
-        for d in range(N):
-            pv(d)
-
-    dve.wait_ge(yd, 1)
-    dve.tensor_copy(T.ysb[:, :], T.yp[:, 0:W]).then_inc(yc, 1)
-    sy.wait_ge(yc, 1)
+        else:
+            pe.wait_ge(T.sem["v%d" % d], vn[d])
+        for h in range(2):
+            if h < len(rs[d]):
+                pe.wait_ge(rs[d][h], 1)
+            i = pe.matmul(Y[h][:, 0:H], lhsT=kv[:, vcols(d)], rhs=T.p[:, d * W + h * H:d * W + (h + 1) * H],
+                          start=(d == 0), stop=(d == N - 1))
+            if d == N - 1:
+                i.then_inc(yd[h], 1)
+    for h in range(2):
+        dve.wait_ge(yd[h], 1)
+        dve.tensor_copy(T.ysb[:, h * H:(h + 1) * H], Y[h][:, 0:H]).then_inc(yc[h], 1)
+        sy.wait_ge(yc[h], 1)
     sy.dma_start(T.y[:, :], T.ysb[:, :]).then_inc(stq, 16)
     sy.wait_ge(stq, 16)

@@ -1,5 +1,5 @@
 from concourse.bass import DstId, RemoteDMATransfer
-from concourse.mybir import AluOpType
+from concourse.mybir import AluOpType, AxisListType, ActivationFunctionType
 
 N = 5
 W = 128
@@ -13,16 +13,15 @@ HOP_AFTER = 1
 SCRATCH = {
     "kv": ("sbuf", [128, N * 2 * W], "bfloat16"),
     "hv": ("sbuf", [128, W], "bfloat16"),
+    "hc": ("sbuf", [128, W], "bfloat16"),
+    "hi": ("sbuf", [128, W], "bfloat16"),
     "qs": ("sbuf", [128, W], "bfloat16"),
-    "ida": ("sbuf", [128, W + 1], "bfloat16"),
-    "dg": ("dram", [W + 1, 128], "bfloat16"),
     "idn": ("sbuf", [128, W], "bfloat16"),
     "zero": ("sbuf", [128, W], "float32"),
     "ones": ("sbuf", [128, W], "bfloat16"),
-    "run": ("sbuf", [128, 2 * N * H], "float32"),
-    "tree": ("sbuf", [128, H], "float32"),
-    "mcol": ("sbuf", [128, 8], "bfloat16"),
-    "mrow": ("sbuf", [128, W], "bfloat16"),
+    "mx": ("sbuf", [128, 4], "float32"),
+    "run": ("sbuf", [128, N * W], "float32"),
+    "dia": ("sbuf", [128, W], "bfloat16"),
     "p": ("sbuf", [128, N * W], "bfloat16"),
     "ysb": ("sbuf", [128, W], "bfloat16"),
     "ps0": ("psum", [128, 512], "float32"),
@@ -34,8 +33,8 @@ SCRATCH = {
     "stb": ("psum", [128, 512], "float32"),
     "yp": ("psum", [128, 512], "float32"),
 }
-SEMAPHORES = (["k%d" % d for d in range(1, N)] + ["v%d" % d for d in range(1, N)] + ["snt", "vin"]
-              + ["c%d" % i for i in range(80)])
+SEMAPHORES = (["k%d" % d for d in range(1, N)] + ["v%d" % d for d in range(1, N)] + ["snt", "vin", "idl"]
+              + ["c%d" % i for i in range(60)])
 
 
 def bits(m):
@@ -89,15 +88,28 @@ def vcols(d):
     return slice(d * 2 * W + W, (d + 1) * 2 * W)
 
 
+def helper_program(g, core, T, topo, r, c, i, nh):
+    wd = W // nh
+    f, a = T.sem.c0, T.sem.c1
+    g.vector.memset(T.hc[:, 0:wd], -0.5).then_inc(f, 1)
+    g.wait_ge(f, 1)
+    g.affine_select(T.hi[:, 0:wd], T.hc[:, 0:wd], [[-1, wd]], AluOpType.is_equal, 0.0, -i * wd, 1).then_inc(a, 1)
+    g.wait_ge(a, 1)
+    m = off_chip(core, T, topo) & topo.mask(core, c)
+    rid, pid, _ = topo.addr(c)
+    g.remote_dma(T.idn[:, i * wd:(i + 1) * wd], T.hi[:, 0:wd], T.sem.idl, T.sem.snt, pid, rid, m)
+    g.wait_ge(T.sem.vin, HOPE)
+    n = fan_out(g, T, topo, core, r, T.hv[:, :], vcols, "v", VGROUPS[i])
+    g.wait_ge(T.sem.snt, n + len(bits(m)))
+
+
 def rank_program(g, core, T, topo):
     rank = T.rank_of(core)
     if rank is None:
         for r, c in enumerate(T.cores):
             hs = helpers_of(c, T, topo)
             if core in hs:
-                g.wait_ge(T.sem.vin, HOPE)
-                n = fan_out(g, T, topo, core, r, T.hv[:, :], vcols, "v", VGROUPS[hs.index(core)])
-                g.wait_ge(T.sem.snt, n)
+                helper_program(g, core, T, topo, r, c, hs.index(core), len(hs))
         return
     pe, dve, sy, sc = g.tensor, g.vector, g.sync, g.scalar
     cnt = [0]
@@ -124,18 +136,12 @@ def rank_program(g, core, T, topo):
     sc.dma_start(kv[:, vcols(0)], T.v[:, :]).then_inc(ldv, 16)
     sc.dma_start(qs[:, :], T.q[:, :]).then_inc(ldq, 16)
 
-    a1, a2, one_s, zero_s, idw, idl = new(), new(), new(), new(), new(), new()
-    dve.memset(T.ida[:, 0:1], -0.5).then_inc(a1, 1)
-    dve.memset(T.ida[:, 1:W + 1], 0.0).then_inc(a2, 1)
-    dve.memset(T.ones[0:1, :], 1.0).then_inc(one_s, 1)
+    one_s, zero_s = new(), new()
+    dve.memset(T.ones[:, :], 1.0).then_inc(one_s, 1)
     dve.memset(T.zero[:, :], 0.0).then_inc(zero_s, 1)
-    sy.wait_ge(a1, 1)
-    sy.wait_ge(a2, 1)
-    sy.dma_start(T.dg[:, :], T.ida[:, :]).then_inc(idw, 16)
-    sy.wait_ge(idw, 16)
-    sy.dma_start(T.idn[:, :], T.dg[0:W, :]).then_inc(idl, 16)
 
     hs = helpers_of(core, T, topo)
+    idn_n = sum(len(bits(off_chip(hc, T, topo) & topo.mask(hc, core))) for hc in hs)
     inner = bits(topo.mask(core, hs[0]) & ~off_chip(core, T, topo))
     hop = []
     for i, hc in enumerate(hs):
@@ -155,63 +161,47 @@ def rank_program(g, core, T, topo):
 
     pe.wait_ge(ldk, 16)
     pe.wait_ge(ldq, 16)
-    rd = [None] * N
-    prev = None
+    t = [None] * N
+    mcol = None
     for d in range(N):
         if d:
             pe.wait_ge(T.sem["k%d" % d], kn[d])
         if d >= 2:
-            pe.wait_ge(rd[d - 2], 1)
+            pe.wait_ge(t[d - 2], 1)
         s = new()
+        t[d] = new()
         pe.matmul(ST[d % 2][:, 0:W], lhsT=qs[:, :], rhs=kv[:, kcols(d)], start=True, stop=True).then_inc(s, 1)
         pe.matmul(S[d][:, 0:W], lhsT=kv[:, kcols(d)], rhs=qs[:, :], start=True, stop=False)
         dve.wait_ge(s, 1)
-        for h in range(2):
-            off = (2 * d + h) * H
-            t = new()
-            if prev is None:
-                dve.tensor_copy(T.run[:, off:off + H], ST[d % 2][:, h * H:(h + 1) * H]).then_inc(t, 1)
-            else:
-                dve.wait_ge(prev[1], 1)
-                dve.tensor_tensor(T.run[:, off:off + H], ST[d % 2][:, h * H:(h + 1) * H],
-                                  T.run[:, prev[0]:prev[0] + H], AluOpType.max).then_inc(t, 1)
-            prev = (off, t)
-        rd[d] = prev[1]
+        if d == 0:
+            dve.tensor_reduce(T.mx[:, 0:1], ST[0][:, 0:W], AxisListType.X, AluOpType.max).then_inc(t[0], 1)
+            mcol = T.mx[:, 0:1]
+        else:
+            if d == 1:
+                dve.wait_ge(zero_s, 1)
+            dve.wait_ge(t[d - 1], 1)
+            dve.tensor_tensor_scan(T.run[:, d * W:(d + 1) * W], ST[d % 2][:, 0:W], T.zero[:, :], mcol,
+                                   AluOpType.max, AluOpType.add).then_inc(t[d], 1)
+            mcol = T.run[:, (d + 1) * W - 1:(d + 1) * W]
 
-    src, so, sem = T.run, prev[0], prev[1]
-    to = 0
-    w = H // 2
-    while w >= 1:
-        t = new()
-        dve.wait_ge(sem, 1)
-        out = T.tree[:, to:to + w] if w > 1 else T.mcol[:, 0:1]
-        dve.tensor_tensor(out, src[:, so:so + w], src[:, so + w:so + 2 * w], AluOpType.max).then_inc(t, 1)
-        src, so, sem = T.tree, to, t
-        to += w
-        w //= 2
-
-    mr, mw = new(), new()
-    pe.wait_ge(idl, 16)
+    dg = new()
+    dve.wait_ge(T.sem.idl, idn_n)
+    dve.wait_ge(t[N - 1], 1)
+    dve.tensor_scalar(T.dia[:, :], T.idn[:, :], mcol, None, AluOpType.mult).then_inc(dg, 1)
     pe.wait_ge(one_s, 1)
-    pe.wait_ge(sem, 1)
-    pe.matmul(T.stb[0:1, 0:W], lhsT=T.mcol[:, 0:1], rhs=T.idn[:, :], start=True, stop=True).then_inc(mr, 1)
-    dve.wait_ge(zero_s, 1)
-    dve.wait_ge(mr, 1)
-    dve.tensor_copy(T.mrow[0:1, :], T.stb[0:1, 0:W]).then_inc(mw, 1)
-    pe.wait_ge(mw, 1)
+    pe.wait_ge(dg, 1)
 
-    rs = {}
+    rs = [None] * N
     for d in range(N):
         b = new()
-        pe.matmul(S[d][:, 0:W], lhsT=T.ones[0:1, :], rhs=T.mrow[0:1, :], start=False, stop=True).then_inc(b, 1)
-        dve.wait_ge(b, 1)
-        parts = [(0, W)] if d < N - 1 else [(0, H), (H, W)]
-        rs[d] = []
-        for lo, hi in parts:
-            r = new()
-            dve.tensor_tensor(T.p[:, d * W + lo:d * W + hi], S[d][:, lo:hi], T.zero[:, lo:hi],
-                              AluOpType.max).then_inc(r, 1)
-            rs[d].append(r)
+        rs[d] = new()
+        pe.matmul(S[d][:, 0:W], lhsT=T.ones[:, :], rhs=T.dia[:, :], start=False, stop=True).then_inc(b, 1)
+        if d % 2 == 0:
+            dve.wait_ge(b, 1)
+            dve.tensor_scalar(T.p[:, d * W:(d + 1) * W], S[d][:, 0:W], 0.0, None, AluOpType.max).then_inc(rs[d], 1)
+        else:
+            sc.wait_ge(b, 1)
+            sc.activation(T.p[:, d * W:(d + 1) * W], S[d][:, 0:W], ActivationFunctionType.Relu).then_inc(rs[d], 1)
 
     yd = [new(), new()]
     yc = [new(), new()]
@@ -221,16 +211,17 @@ def rank_program(g, core, T, topo):
             pe.wait_ge(ldv, 16)
         else:
             pe.wait_ge(T.sem["v%d" % d], vn[d])
+        pe.wait_ge(rs[d], 1)
         for h in range(2):
-            if h < len(rs[d]):
-                pe.wait_ge(rs[d][h], 1)
             i = pe.matmul(Y[h][:, 0:H], lhsT=kv[:, vcols(d)], rhs=T.p[:, d * W + h * H:d * W + (h + 1) * H],
                           start=(d == 0), stop=(d == N - 1))
             if d == N - 1:
                 i.then_inc(yd[h], 1)
-    for h in range(2):
-        dve.wait_ge(yd[h], 1)
-        dve.tensor_copy(T.ysb[:, h * H:(h + 1) * H], Y[h][:, 0:H]).then_inc(yc[h], 1)
-        sy.wait_ge(yc[h], 1)
+    dve.wait_ge(yd[0], 1)
+    dve.tensor_copy(T.ysb[:, 0:H], Y[0][:, 0:H]).then_inc(yc[0], 1)
+    sc.wait_ge(yd[1], 1)
+    sc.activation(T.ysb[:, H:W], Y[1][:, 0:H], ActivationFunctionType.Copy).then_inc(yc[1], 1)
+    sy.wait_ge(yc[0], 1)
+    sy.wait_ge(yc[1], 1)
     sy.dma_start(T.y[:, :], T.ysb[:, :]).then_inc(stq, 16)
     sy.wait_ge(stq, 16)

@@ -11,17 +11,18 @@ HOPE = 4
 HOP_AFTER = 1
 
 SCRATCH = {
+    "kd": ("dram", [128, W], "bfloat16"),
+    "vd": ("dram", [128, W], "bfloat16"),
+    "hvd": ("dram", [128, W], "bfloat16"),
     "kv": ("sbuf", [128, N * 2 * W], "bfloat16"),
-    "hv": ("sbuf", [128, W], "bfloat16"),
     "hc": ("sbuf", [128, W], "bfloat16"),
     "hi": ("sbuf", [128, W], "bfloat16"),
     "qs": ("sbuf", [128, W], "bfloat16"),
     "idn": ("sbuf", [128, W], "bfloat16"),
-    "zero": ("sbuf", [128, W], "float32"),
-    "ones": ("sbuf", [128, W], "bfloat16"),
+    "zero": ("sbuf", [128, 2 * W], "float32"),
     "mx": ("sbuf", [128, 4], "float32"),
     "run": ("sbuf", [128, N * W], "float32"),
-    "dia": ("sbuf", [128, W], "bfloat16"),
+    "mb": ("sbuf", [128, 2 * W], "bfloat16"),
     "p": ("sbuf", [128, N * W], "bfloat16"),
     "ysb": ("sbuf", [128, W], "bfloat16"),
     "ps0": ("psum", [128, 512], "float32"),
@@ -99,7 +100,7 @@ def helper_program(g, core, T, topo, r, c, i, nh):
     rid, pid, _ = topo.addr(c)
     g.remote_dma(T.idn[:, i * wd:(i + 1) * wd], T.hi[:, 0:wd], T.sem.idl, T.sem.snt, pid, rid, m)
     g.wait_ge(T.sem.vin, HOPE)
-    n = fan_out(g, T, topo, core, r, T.hv[:, :], vcols, "v", VGROUPS[i])
+    n = fan_out(g, T, topo, core, r, T.hvd[:, :], vcols, "v", VGROUPS[i])
     g.wait_ge(T.sem.snt, n + len(bits(m)))
 
 
@@ -121,7 +122,7 @@ def rank_program(g, core, T, topo):
 
     kv, qs = T.kv, T.qs
     S = [T.ps0, T.ps1, T.ps2, T.ps3, T.ps4]
-    ST = [T.sta, T.stb]
+    ST = [T.sta[:, 0:W], T.stb[:, 0:W], T.sta[:, W:2 * W], T.stb[:, 0:W], T.sta[:, 0:W]]
     Y = [T.yp, T.sta]
     kn, vn = {}, {}
     for grp in KGROUPS:
@@ -131,13 +132,14 @@ def rank_program(g, core, T, topo):
         for d in grp:
             vn[d] = share(grp, core, T, topo)
 
-    ldk, ldv, ldq = new(), new(), new()
+    ldd, lde, ldk, ldv, ldq = new(), new(), new(), new(), new()
+    sy.dma_start(T.kd[:, :], T.k[:, :]).then_inc(ldd, 16)
+    sc.dma_start(T.vd[:, :], T.v[:, :]).then_inc(lde, 16)
     sy.dma_start(kv[:, kcols(0)], T.k[:, :]).then_inc(ldk, 16)
-    sc.dma_start(kv[:, vcols(0)], T.v[:, :]).then_inc(ldv, 16)
     sc.dma_start(qs[:, :], T.q[:, :]).then_inc(ldq, 16)
+    sc.dma_start(kv[:, vcols(0)], T.v[:, :]).then_inc(ldv, 16)
 
-    one_s, zero_s = new(), new()
-    dve.memset(T.ones[:, :], 1.0).then_inc(one_s, 1)
+    zero_s = new()
     dve.memset(T.zero[:, :], 0.0).then_inc(zero_s, 1)
 
     hs = helpers_of(core, T, topo)
@@ -148,15 +150,15 @@ def rank_program(g, core, T, topo):
         rid, pid, _ = topo.addr(hc)
         hop.append(RemoteDMATransfer(dst_ids=[DstId(rid=rid, pnc=pid)],
                                      dma_engine_mask=tomask(inner[i * HOPE:(i + 1) * HOPE]),
-                                     remote_sem=T.sem.vin, src=kv[:, vcols(0)], dst=T.hv[:, :]))
+                                     remote_sem=T.sem.vin, src=T.vd[:, :], dst=T.hvd[:, :]))
     sent = 0
-    g.wait_ge(ldk, 16)
+    g.wait_ge(ldd, 16)
     for n, grp in enumerate(KGROUPS):
         if n == HOP_AFTER:
-            g.wait_ge(ldv, 16)
+            g.wait_ge(lde, 16)
             g.remote_dma_fused(hop, local_sem=T.sem.snt)
             sent += HOPE * len(hs)
-        sent += fan_out(g, T, topo, core, rank, kv[:, kcols(0)], kcols, "k", grp)
+        sent += fan_out(g, T, topo, core, rank, T.kd[:, :], kcols, "k", grp)
     g.wait_ge(T.sem.snt, sent)
 
     pe.wait_ge(ldk, 16)
@@ -170,32 +172,31 @@ def rank_program(g, core, T, topo):
             pe.wait_ge(t[d - 2], 1)
         s = new()
         t[d] = new()
-        pe.matmul(ST[d % 2][:, 0:W], lhsT=qs[:, :], rhs=kv[:, kcols(d)], start=True, stop=True).then_inc(s, 1)
+        pe.matmul(ST[d], lhsT=qs[:, :], rhs=kv[:, kcols(d)], start=True, stop=True).then_inc(s, 1)
         pe.matmul(S[d][:, 0:W], lhsT=kv[:, kcols(d)], rhs=qs[:, :], start=True, stop=False)
         dve.wait_ge(s, 1)
         if d == 0:
-            dve.tensor_reduce(T.mx[:, 0:1], ST[0][:, 0:W], AxisListType.X, AluOpType.max).then_inc(t[0], 1)
+            dve.tensor_reduce(T.mx[:, 0:1], ST[0], AxisListType.X, AluOpType.max).then_inc(t[0], 1)
             mcol = T.mx[:, 0:1]
-        else:
+        elif d < N - 1:
             if d == 1:
                 dve.wait_ge(zero_s, 1)
             dve.wait_ge(t[d - 1], 1)
-            dve.tensor_tensor_scan(T.run[:, d * W:(d + 1) * W], ST[d % 2][:, 0:W], T.zero[:, :], mcol,
+            dve.tensor_tensor_scan(T.run[:, d * W:(d + 1) * W], ST[d], T.zero[:, 0:W], mcol,
                                    AluOpType.max, AluOpType.add).then_inc(t[d], 1)
             mcol = T.run[:, (d + 1) * W - 1:(d + 1) * W]
+        else:
+            dve.wait_ge(t[d - 1], 1)
+            dve.tensor_tensor_scan(T.mb[:, :], T.sta[:, 0:2 * W], T.zero[:, :], mcol,
+                                   AluOpType.max, AluOpType.add).then_inc(t[d], 1)
 
-    dg = new()
-    dve.wait_ge(T.sem.idl, idn_n)
-    dve.wait_ge(t[N - 1], 1)
-    dve.tensor_scalar(T.dia[:, :], T.idn[:, :], mcol, None, AluOpType.mult).then_inc(dg, 1)
-    pe.wait_ge(one_s, 1)
-    pe.wait_ge(dg, 1)
-
+    pe.wait_ge(T.sem.idl, idn_n)
+    pe.wait_ge(t[N - 1], 1)
     rs = [None] * N
     for d in range(N):
         b = new()
         rs[d] = new()
-        pe.matmul(S[d][:, 0:W], lhsT=T.ones[:, :], rhs=T.dia[:, :], start=False, stop=True).then_inc(b, 1)
+        pe.matmul(S[d][:, 0:W], lhsT=T.mb[:, W:2 * W], rhs=T.idn[:, :], start=False, stop=True).then_inc(b, 1)
         if d % 2 == 0:
             dve.wait_ge(b, 1)
             dve.tensor_scalar(T.p[:, d * W:(d + 1) * W], S[d][:, 0:W], 0.0, None, AluOpType.max).then_inc(rs[d], 1)

@@ -9,6 +9,7 @@ KGROUPS = [[1, 2], [3], [4]]
 VGROUPS = [[1, 2], [3, 4]]
 HOPE = 4
 HOP_AFTER = 1
+RW = 16
 
 SCRATCH = {
     "kd": ("dram", [128, W], "bfloat16"),
@@ -17,6 +18,8 @@ SCRATCH = {
     "kv": ("sbuf", [128, N * 2 * W], "bfloat16"),
     "hc": ("sbuf", [128, W], "bfloat16"),
     "hi": ("sbuf", [128, W], "bfloat16"),
+    "rs": ("sbuf", [128, RW], "bfloat16"),
+    "rmp": ("sbuf", [128, RW], "bfloat16"),
     "qs": ("sbuf", [128, W], "bfloat16"),
     "idn": ("sbuf", [128, W], "bfloat16"),
     "zero": ("sbuf", [128, 2 * W], "float32"),
@@ -34,7 +37,7 @@ SCRATCH = {
     "stb": ("psum", [128, 512], "float32"),
     "yp": ("psum", [128, 512], "float32"),
 }
-SEMAPHORES = (["k%d" % d for d in range(1, N)] + ["v%d" % d for d in range(1, N)] + ["snt", "vin", "idl"]
+SEMAPHORES = (["k%d" % d for d in range(1, N)] + ["v%d" % d for d in range(1, N)] + ["snt", "vin", "idl", "rin"]
               + ["c%d" % i for i in range(60)])
 
 
@@ -90,15 +93,16 @@ def vcols(d):
 
 
 def helper_program(g, core, T, topo, r, c, i, nh):
-    wd = W // nh
+    wd = (W - RW) // nh
+    off = RW + i * wd
     f, a = T.sem.c0, T.sem.c1
     g.vector.memset(T.hc[:, 0:wd], -0.5).then_inc(f, 1)
     g.wait_ge(f, 1)
-    g.affine_select(T.hi[:, 0:wd], T.hc[:, 0:wd], [[-1, wd]], AluOpType.is_equal, 0.0, -i * wd, 1).then_inc(a, 1)
+    g.affine_select(T.hi[:, 0:wd], T.hc[:, 0:wd], [[-1, wd]], AluOpType.is_equal, 0.0, -off, 1).then_inc(a, 1)
     g.wait_ge(a, 1)
     m = off_chip(core, T, topo) & topo.mask(core, c)
     rid, pid, _ = topo.addr(c)
-    g.remote_dma(T.idn[:, i * wd:(i + 1) * wd], T.hi[:, 0:wd], T.sem.idl, T.sem.snt, pid, rid, m)
+    g.remote_dma(T.idn[:, off:off + wd], T.hi[:, 0:wd], T.sem.idl, T.sem.snt, pid, rid, m)
     g.wait_ge(T.sem.vin, HOPE)
     n = fan_out(g, T, topo, core, r, T.hvd[:, :], vcols, "v", VGROUPS[i])
     g.wait_ge(T.sem.snt, n + len(bits(m)))
@@ -144,7 +148,8 @@ def rank_program(g, core, T, topo):
 
     hs = helpers_of(core, T, topo)
     idn_n = sum(len(bits(off_chip(hc, T, topo) & topo.mask(hc, core))) for hc in hs)
-    inner = bits(topo.mask(core, hs[0]) & ~off_chip(core, T, topo))
+    om = off_chip(core, T, topo)
+    inner = bits(topo.mask(core, hs[0]) & ~om)
     hop = []
     for i, hc in enumerate(hs):
         rid, pid, _ = topo.addr(hc)
@@ -152,6 +157,12 @@ def rank_program(g, core, T, topo):
                                      dma_engine_mask=tomask(inner[i * HOPE:(i + 1) * HOPE]),
                                      remote_sem=T.sem.vin, src=T.vd[:, :], dst=T.hvd[:, :]))
     sent = 0
+    io = new()
+    g.iota(T.rs[:, :], [[-1, RW]], 0, 1, allow_small_or_imprecise_dtypes=True).then_inc(io, 1)
+    g.wait_ge(io, 1)
+    rid, pid, _ = topo.addr(T.cores[(rank + 1) % N])
+    g.remote_dma(T.rmp[:, :], T.rs[:, :], T.sem.rin, T.sem.snt, pid, rid, om)
+    sent += len(bits(om))
     g.wait_ge(ldd, 16)
     for n, grp in enumerate(KGROUPS):
         if n == HOP_AFTER:
@@ -165,6 +176,7 @@ def rank_program(g, core, T, topo):
     pe.wait_ge(ldq, 16)
     t = [None] * N
     mcol = None
+    idv = new()
     for d in range(N):
         if d:
             pe.wait_ge(T.sem["k%d" % d], kn[d])
@@ -173,11 +185,15 @@ def rank_program(g, core, T, topo):
         s = new()
         t[d] = new()
         pe.matmul(ST[d], lhsT=qs[:, :], rhs=kv[:, kcols(d)], start=True, stop=True).then_inc(s, 1)
-        pe.matmul(S[d][:, 0:W], lhsT=kv[:, kcols(d)], rhs=qs[:, :], start=True, stop=False)
+        for e in ([d] if d < N - 2 else [] if d == N - 2 else [N - 2, N - 1]):
+            pe.matmul(S[e][:, 0:W], lhsT=kv[:, kcols(e)], rhs=qs[:, :], start=True, stop=False)
         dve.wait_ge(s, 1)
         if d == 0:
             dve.tensor_reduce(T.mx[:, 0:1], ST[0], AxisListType.X, AluOpType.max).then_inc(t[0], 1)
             mcol = T.mx[:, 0:1]
+            dve.wait_ge(T.sem.rin, len(bits(om)))
+            dve.tensor_scalar(T.idn[:, 0:RW], T.rmp[:, :], 0.0, -0.5, AluOpType.is_equal,
+                              AluOpType.mult).then_inc(idv, 1)
         elif d < N - 1:
             if d == 1:
                 dve.wait_ge(zero_s, 1)
@@ -191,6 +207,7 @@ def rank_program(g, core, T, topo):
                                    AluOpType.max, AluOpType.add).then_inc(t[d], 1)
 
     pe.wait_ge(T.sem.idl, idn_n)
+    pe.wait_ge(idv, 1)
     pe.wait_ge(t[N - 1], 1)
     rs = [None] * N
     for d in range(N):

from concourse.bass import DstId, RemoteDMATransfer
from concourse.mybir import AluOpType, AxisListType, ActivationFunctionType

N = 5
W = 128
H = W // 2
SIM = 96
KGROUPS = [[1, 2], [3], [4]]
VGROUPS = [[1, 2], [3, 4]]
HOPE = 4
HOP_AFTER = 1
RW = 16

SCRATCH = {
    "kd": ("dram", [128, W], "bfloat16"),
    "vd": ("dram", [128, W], "bfloat16"),
    "hvd": ("dram", [128, W], "bfloat16"),
    "kv": ("sbuf", [128, N * 2 * W], "bfloat16"),
    "hc": ("sbuf", [128, W], "bfloat16"),
    "hi": ("sbuf", [128, W], "bfloat16"),
    "rs": ("sbuf", [128, RW], "bfloat16"),
    "rmp": ("sbuf", [128, RW], "bfloat16"),
    "qs": ("sbuf", [128, W], "bfloat16"),
    "idn": ("sbuf", [128, W], "bfloat16"),
    "zero": ("sbuf", [128, 2 * W], "float32"),
    "mx": ("sbuf", [128, 4], "float32"),
    "run": ("sbuf", [128, N * W], "float32"),
    "mb": ("sbuf", [128, 2 * W], "bfloat16"),
    "p": ("sbuf", [128, N * W], "bfloat16"),
    "ysb": ("sbuf", [128, W], "bfloat16"),
    "ps0": ("psum", [128, 512], "float32"),
    "ps1": ("psum", [128, 512], "float32"),
    "ps2": ("psum", [128, 512], "float32"),
    "ps3": ("psum", [128, 512], "float32"),
    "ps4": ("psum", [128, 512], "float32"),
    "sta": ("psum", [128, 512], "float32"),
    "stb": ("psum", [128, 512], "float32"),
    "yp": ("psum", [128, 512], "float32"),
}
SEMAPHORES = (["k%d" % d for d in range(1, N)] + ["v%d" % d for d in range(1, N)] + ["snt", "vin", "idl", "rin"]
              + ["c%d" % i for i in range(60)])


def bits(m):
    return [e for e in range(16) if (m >> e) & 1]


def tomask(es):
    m = 0
    for e in es:
        m |= 1 << e
    return m


def helpers_of(c, T, topo):
    hs = [h for h in range(SIM) if h != c and topo.chip(h) == topo.chip(c) and topo.die(h) != topo.die(c)
          and all(topo.may_write(h, x) for x in T.cores)]
    return hs[:len(VGROUPS)]


def off_chip(core, T, topo):
    m = None
    for c in T.cores:
        if topo.chip(c) != topo.chip(core):
            m = topo.mask(core, c) if m is None else m & topo.mask(core, c)
    return m


def share(group, core, T, topo):
    return len(bits(off_chip(core, T, topo))) // len(group)


def fan_out(g, T, topo, core, rank, src, cols_of, semname, group):
    engines = bits(off_chip(core, T, topo))
    ne = len(engines) // len(group)
    trs = []
    for i, d in enumerate(group):
        rid, pid, _ = topo.addr(T.cores[(rank + d) % N])
        trs.append(RemoteDMATransfer(dst_ids=[DstId(rid=rid, pnc=pid)],
                                     dma_engine_mask=tomask(engines[i * ne:(i + 1) * ne]),
                                     remote_sem=T.sem["%s%d" % (semname, d)],
                                     src=src, dst=T.kv[:, cols_of(d)]))
    g.remote_dma_fused(trs, local_sem=T.sem.snt)
    return ne * len(group)


def kcols(d):
    return slice(d * 2 * W, d * 2 * W + W)


def vcols(d):
    return slice(d * 2 * W + W, (d + 1) * 2 * W)


def helper_program(g, core, T, topo, r, c, i, nh):
    wd = (W - RW) // nh
    off = RW + i * wd
    f, a = T.sem.c0, T.sem.c1
    g.vector.memset(T.hc[:, 0:wd], -0.5).then_inc(f, 1)
    g.wait_ge(f, 1)
    g.affine_select(T.hi[:, 0:wd], T.hc[:, 0:wd], [[-1, wd]], AluOpType.is_equal, 0.0, -off, 1).then_inc(a, 1)
    g.wait_ge(a, 1)
    m = off_chip(core, T, topo) & topo.mask(core, c)
    rid, pid, _ = topo.addr(c)
    g.remote_dma(T.idn[:, off:off + wd], T.hi[:, 0:wd], T.sem.idl, T.sem.snt, pid, rid, m)
    g.wait_ge(T.sem.vin, HOPE)
    n = fan_out(g, T, topo, core, r, T.hvd[:, :], vcols, "v", VGROUPS[i])
    g.wait_ge(T.sem.snt, n + len(bits(m)))


def rank_program(g, core, T, topo):
    rank = T.rank_of(core)
    if rank is None:
        for r, c in enumerate(T.cores):
            hs = helpers_of(c, T, topo)
            if core in hs:
                helper_program(g, core, T, topo, r, c, hs.index(core), len(hs))
        return
    pe, dve, sy, sc = g.tensor, g.vector, g.sync, g.scalar
    cnt = [0]

    def new():
        s = T.sem["c%d" % cnt[0]]
        cnt[0] += 1
        return s

    kv, qs = T.kv, T.qs
    S = [T.ps0, T.ps1, T.ps2, T.ps3, T.ps4]
    ST = [T.sta[:, 0:W], T.stb[:, 0:W], T.sta[:, W:2 * W], T.stb[:, 0:W], T.sta[:, 0:W]]
    Y = [T.yp, T.sta]
    kn, vn = {}, {}
    for grp in KGROUPS:
        for d in grp:
            kn[d] = share(grp, core, T, topo)
    for grp in VGROUPS:
        for d in grp:
            vn[d] = share(grp, core, T, topo)

    ldd, lde, ldk, ldv, ldq = new(), new(), new(), new(), new()
    sy.dma_start(T.kd[:, :], T.k[:, :]).then_inc(ldd, 16)
    sc.dma_start(T.vd[:, :], T.v[:, :]).then_inc(lde, 16)
    sy.dma_start(kv[:, kcols(0)], T.k[:, :]).then_inc(ldk, 16)
    sc.dma_start(qs[:, :], T.q[:, :]).then_inc(ldq, 16)
    sc.dma_start(kv[:, vcols(0)], T.v[:, :]).then_inc(ldv, 16)

    zero_s = new()
    dve.memset(T.zero[:, :], 0.0).then_inc(zero_s, 1)

    hs = helpers_of(core, T, topo)
    idn_n = sum(len(bits(off_chip(hc, T, topo) & topo.mask(hc, core))) for hc in hs)
    om = off_chip(core, T, topo)
    inner = bits(topo.mask(core, hs[0]) & ~om)
    hop = []
    for i, hc in enumerate(hs):
        rid, pid, _ = topo.addr(hc)
        hop.append(RemoteDMATransfer(dst_ids=[DstId(rid=rid, pnc=pid)],
                                     dma_engine_mask=tomask(inner[i * HOPE:(i + 1) * HOPE]),
                                     remote_sem=T.sem.vin, src=T.vd[:, :], dst=T.hvd[:, :]))
    sent = 0
    io = new()
    g.iota(T.rs[:, :], [[-1, RW]], 0, 1, allow_small_or_imprecise_dtypes=True).then_inc(io, 1)
    g.wait_ge(io, 1)
    rid, pid, _ = topo.addr(T.cores[(rank + 1) % N])
    g.remote_dma(T.rmp[:, :], T.rs[:, :], T.sem.rin, T.sem.snt, pid, rid, om)
    sent += len(bits(om))
    g.wait_ge(ldd, 16)
    for n, grp in enumerate(KGROUPS):
        if n == HOP_AFTER:
            g.wait_ge(lde, 16)
            g.remote_dma_fused(hop, local_sem=T.sem.snt)
            sent += HOPE * len(hs)
        sent += fan_out(g, T, topo, core, rank, T.kd[:, :], kcols, "k", grp)
    g.wait_ge(T.sem.snt, sent)

    pe.wait_ge(ldk, 16)
    pe.wait_ge(ldq, 16)
    t = [None] * N
    mcol = None
    idv = new()
    for d in range(N):
        if d:
            pe.wait_ge(T.sem["k%d" % d], kn[d])
        if d >= 2:
            pe.wait_ge(t[d - 2], 1)
        s = new()
        t[d] = new()
        pe.matmul(ST[d], lhsT=qs[:, :], rhs=kv[:, kcols(d)], start=True, stop=True).then_inc(s, 1)
        for e in ([d] if d < N - 2 else [] if d == N - 2 else [N - 2, N - 1]):
            pe.matmul(S[e][:, 0:W], lhsT=kv[:, kcols(e)], rhs=qs[:, :], start=True, stop=False)
        dve.wait_ge(s, 1)
        if d == 0:
            dve.tensor_reduce(T.mx[:, 0:1], ST[0], AxisListType.X, AluOpType.max).then_inc(t[0], 1)
            mcol = T.mx[:, 0:1]
            dve.wait_ge(T.sem.rin, len(bits(om)))
            dve.tensor_scalar(T.idn[:, 0:RW], T.rmp[:, :], 0.0, -0.5, AluOpType.is_equal,
                              AluOpType.mult).then_inc(idv, 1)
        elif d < N - 1:
            if d == 1:
                dve.wait_ge(zero_s, 1)
            dve.wait_ge(t[d - 1], 1)
            dve.tensor_tensor_scan(T.run[:, d * W:(d + 1) * W], ST[d], T.zero[:, 0:W], mcol,
                                   AluOpType.max, AluOpType.add).then_inc(t[d], 1)
            mcol = T.run[:, (d + 1) * W - 1:(d + 1) * W]
        else:
            dve.wait_ge(t[d - 1], 1)
            dve.tensor_tensor_scan(T.mb[:, :], T.sta[:, 0:2 * W], T.zero[:, :], mcol,
                                   AluOpType.max, AluOpType.add).then_inc(t[d], 1)

    pe.wait_ge(T.sem.idl, idn_n)
    pe.wait_ge(idv, 1)
    pe.wait_ge(t[N - 1], 1)
    rs = [None] * N
    for d in range(N):
        b = new()
        rs[d] = new()
        pe.matmul(S[d][:, 0:W], lhsT=T.mb[:, W:2 * W], rhs=T.idn[:, :], start=False, stop=True).then_inc(b, 1)
        if d % 2 == 0:
            dve.wait_ge(b, 1)
            dve.tensor_scalar(T.p[:, d * W:(d + 1) * W], S[d][:, 0:W], 0.0, None, AluOpType.max).then_inc(rs[d], 1)
        else:
            sc.wait_ge(b, 1)
            sc.activation(T.p[:, d * W:(d + 1) * W], S[d][:, 0:W], ActivationFunctionType.Relu).then_inc(rs[d], 1)

    yd = [new(), new()]
    yc = [new(), new()]
    stq = new()
    for d in range(N):
        if d == 0:
            pe.wait_ge(ldv, 16)
        else:
            pe.wait_ge(T.sem["v%d" % d], vn[d])
        pe.wait_ge(rs[d], 1)
        for h in range(2):
            i = pe.matmul(Y[h][:, 0:H], lhsT=kv[:, vcols(d)], rhs=T.p[:, d * W + h * H:d * W + (h + 1) * H],
                          start=(d == 0), stop=(d == N - 1))
            if d == N - 1:
                i.then_inc(yd[h], 1)
    dve.wait_ge(yd[0], 1)
    dve.tensor_copy(T.ysb[:, 0:H], Y[0][:, 0:H]).then_inc(yc[0], 1)
    sc.wait_ge(yd[1], 1)
    sc.activation(T.ysb[:, H:W], Y[1][:, 0:H], ActivationFunctionType.Copy).then_inc(yc[1], 1)
    sy.wait_ge(yc[0], 1)
    sy.wait_ge(yc[1], 1)
    sy.dma_start(T.y[:, :], T.ysb[:, :]).then_inc(stq, 16)
    sy.wait_ge(stq, 16)
